import numpy as np, ml_dtypes
CORES = [1,5,17,21,33,37,49,53]
N = 8
import mx_ref
BF = ml_dtypes.bfloat16
def tile(rs):
    return np.stack(rs, axis=2).reshape(128, -1).astype(BF)
def pick(q, e):
    c = np.concatenate([q[0].reshape(128, -1, 4), np.zeros((128, 1, 4), np.uint8)], axis=1); s = np.concatenate([q[1], np.ones((16, 1), np.uint8)], axis=1)
    return (np.ascontiguousarray(c[:, e].reshape(128, -1)), np.ascontiguousarray(s[:, e]))
def join(*qs):
    return (np.concatenate([q[0] for q in qs], axis=1), np.concatenate([q[1] for q in qs], axis=1))
def put(q, e, v):
    c, s = q[0].reshape(128, -1, 4).copy(), q[1].copy(); c[:, e] = v[0].reshape(128, -1, 4); s[:, e] = v[1]
    return (c.reshape(128, -1), s)
def pk(c, s):
    return (np.ascontiguousarray(c), mx_ref.live(s))
def emit(q):
    return q[0], q[1]
def packed(v, rng):
    q = [mx_ref.quantize(np.ascontiguousarray(v[r])) for r in range(N)]
    return np.stack([a for a, b in q]), np.stack([mx_ref.plane(b, rng) for a, b in q])
def values_of_codes():
    e, c = np.zeros((128, 128, 4), np.float32), np.zeros((128, 2, 4), np.uint8)
    e[np.arange(128), np.arange(128), 0] = 1
    c[:127, :, 0] = np.arange(256).reshape(2, 128).T[:127]
    return mx_ref.matmul(mx_ref.quantize(e.reshape(128, 512).astype(BF)), (c.reshape(128, 8), np.full((16, 2), 127, np.uint8))).T.reshape(-1).astype(np.float64)
CODE_VALUE, SCALE_VALUE = values_of_codes(), 2.0 ** (np.arange(256) - 127.0)
def decode(q):
    return (CODE_VALUE[q[0]].reshape(16, 8, -1, 4) * SCALE_VALUE[q[1]][:, None, :, None] + 0.0).reshape(128, -1).astype(np.float32)
def f(rng, *shape):
    return mx_ref.flush((rng.standard_normal(shape, dtype=np.float32) * np.exp2(rng.integers(-2, 3, shape[:-1] + (1,)))).astype(BF))
def wide(rng, *shape, cols=0):
    v = rng.standard_normal(shape, dtype=np.float32) * np.exp2(rng.integers(-12, 13, shape)).astype(np.float32)
    if cols: v *= np.repeat(np.exp2(rng.integers(-cols, cols + 1, shape[:-2] + (1, shape[-1] // 4))) * (rng.random(shape[:-2] + (1, shape[-1] // 4)) > 0.0625), 4, axis=-1).astype(np.float32)
    return mx_ref.flush(v.astype(BF))
C, H = 256, 128
MASK = [1, 2, 4]
def numbers_of(rng):
    return {"x": np.array(f(rng, N, 128, 4 * C)), "u": np.array(f(rng, N, 128, 512)), "v": np.array(f(rng, N, 128, 512))}
def layers(rng, still=[]):
    w = np.array(mx_ref.flush((np.clip(f(rng, N, 128, 2048).astype(np.float32), -4, 4) * np.float32(0.125)).astype(BF))).reshape(N, 8, 16, 4, 8, 16, 4)
    for i in still: w[:, :, :, :, :, i] = 0
    return w
def weights(rng, w):
    c, p = packed(np.ascontiguousarray(w).reshape(N, 128, 2048), rng)
    return {"wc": c, "ws": p}
def setup_inputs(rng):
    return {**numbers_of(rng), **weights(rng, layers(rng))}
def setup_inputs_ties(rng):
    d = numbers_of(rng)
    o = rng.permutation(N)
    x = d["x"].reshape(N, 8, 16, C, 4)
    k = rng.integers(0, 3, (N, 8, C)) - 4 * (o % 2)[:, None, None]
    k[o == 2] = np.arange(8)[:, None]
    x[:, :, 0] = 0
    x[:, :, 0, :, 0] = k.astype(np.float32).astype(BF)
    z = 1 + 32 * rng.permutation(C // 32)[np.arange(C) // 32] + rng.permutation(32)[np.arange(C) % 32]
    z = 4 * z[None, :] + ((np.arange(8) + int(rng.choice([2, 4, 6]))) % 8 // 2)[:, None]
    for r in range(N):
        if o[r] == 3: x[r, :, 0] = (-((z[:, :, None] >> (3 * np.arange(4))) & 7)).astype(np.float32).astype(BF)
    n = (N, 8, 8, C, 4)
    a = (129 + 2 * rng.integers(0, 64, n)) * np.exp2(-7.0 - rng.integers(8, 15, n)) * (rng.integers(0, 2, n) * 2.0 - 1.0)
    a[:, :, 0, :, 0] = 1.96875
    a = a * np.exp2(1.0 * rng.integers(-2, 3, (N, 8, 1, C, 1)))
    x[:, :, 8:] = a.astype(np.float32).astype(BF)
    u = d["u"].reshape(N, 128, 128, 4)
    u[:, :, ::16] = 0
    for r in range(N):
        for h in range(0, 128, 16):
            u[r, h, h, 0] = 0.0 if o[r] == 0 else -1.0 if o[r] == 1 else 1.0
            if o[r] == 3: u[r, h, h] = np.exp2(3.0 * np.arange(4)).astype(np.float32).astype(BF)
    return {"x": x.reshape(N, 128, 4 * C), "u": u.reshape(N, 128, 512), "v": d["v"], **weights(rng, layers(rng, [0] + [*range(8, 16)]))}
def setup_inputs_near(rng):
    d = numbers_of(rng)
    x = d["x"].astype(np.float32).reshape(N, 8, 16, C, 4)
    x[:, :, 0] = 0
    x[:, :, 8:] = 0
    u = d["u"].reshape(N, 128, 128, 4)
    u[:, :, ::16] = 0
    o = rng.permutation(N) % 4
    for r in range(N):
        s = rng.integers(0, 16, (8, C, 1))
        if o[r] < 3: x[r, :, 8] = ((s >> np.arange(4)) & 1) * np.exp2(np.arange(4) - 23.0)
        if o[r] < 2:
            x[r, :, 0, :, 0] = rng.integers(0, 2, (8, C)) * 2.0 - 1.0
            x[r, :, 11, :, 0] = 2.0 ** -10
        if o[r] == 2:
            e = rng.permutation(8)
            x[r, e[0], 0, :, 0] = 1.0
            x[r, e[1], 0, :, 0] = -1.0
        if o[r] == 3:
            x[r, :4, 10, :, 0] = rng.choice([1.0, 2.0], (4, C)) * 2.0 ** -30
            x[r, 4:, 10, :, 0] = rng.choice([1.125, 2.0], (4, C)) * 2.0 ** -30
            t = rng.permutation(C)[:C // 4]
            z = rng.integers(0, 2, (8, C // 4)) * 0.25
            c = np.where(np.arange(8) < 4, 1.0, 1.125)[:, None]
            x[r][:, 10, t, 0] = (c + z) * 2.0 ** -30
            x[r][:, 12, t, 0] = (c - z - 2.125) * 2.0 ** -30
        k = 1.0 if o[r] == 0 else 2.0 ** -30
        for h in range(0, 128, 16):
            u[r, h, h, 0] = 1.0 if o[r] == 2 else k
            u[r, h + 8, h] = k
            u[r, h + 11, h, 0] = k
            u[r, h + 10, h, 0] = k if o[r] < 3 else k * 1.25 if h < 64 else k * 1.125
            u[r, h + 12, h, 0] = 0.0 if o[r] < 3 else k * 1.125 if h < 64 else k * 1.25
    return {"x": x.reshape(N, 128, 4 * C).astype(BF), "u": u.reshape(N, 128, 512), "v": d["v"], **weights(rng, layers(rng, [0] + [*range(8, 16)]))}
def setup_inputs_huge(rng):
    d = numbers_of(rng)
    o = rng.permutation(N) % 2
    c = rng.integers(0, 2, (N, 1, 1, C, 1)) * 2.0 - 1.0
    c[o == 0] = -1.0
    x = (0.6 + 0.08 * rng.random((N, 8, 16, C, 4))) * 2.0 ** 30 * c
    a = 2.0 ** 30 * (1.0 - 0.1 * rng.random((N, 128, 8, 4)))
    a[o == 1] *= rng.choice([-1.0, 1.0], (N // 2, 1, 8, 1))
    u = d["u"].reshape(N, 128, 128, 4)
    u[:, :, ::16] = a.astype(np.float32).astype(BF)
    w = rng.integers(1, 3, (N, 8, 16, 4, 8, 16, 4)) * 2.0 ** -9 * rng.choice([-1.0, 1.0], (N, 1, 1, 4, 8, 16, 1))
    return {"x": x.astype(np.float32).reshape(N, 128, 4 * C).astype(BF), "u": u.reshape(N, 128, 512), "v": d["v"], **weights(rng, w.astype(np.float32).astype(BF))}
def setup_inputs_ends(rng):
    d = numbers_of(rng)
    o = rng.permutation(N) % 4
    most, least = 255.0 * 2.0 ** 22, 2.0 ** -30
    x = np.full((N, 8, C), least)
    u = d["u"].reshape(N, 8, 16, 128, 4)
    v = rng.choice([-1.0, 1.0], (N, 128, 512))
    for r in range(N):
        a = np.ones((8, 16, 8, 4)) * (2.0 ** -30 if o[r] == 2 else 2.0 ** 30)
        if o[r] == 0:
            x[r] = -most
            for g in rng.permutation(8)[:4]: a[:, :, g] *= rng.choice([0.5, 1.0], (8, 16, 4))
        else: a *= rng.choice([-1.0, 1.0], (8, 1, 8, 1))
        if o[r] == 1: x[r] = most * rng.choice([-1.0, 1.0], (1, C))
        if o[r] == 3: x[r] = np.where(rng.random((8, C)) < 0.5, least, most * rng.choice([-1.0, 1.0], (8, C)))
        u[r][:, :, ::16] = a.astype(np.float32).astype(BF)
        v[r] *= 2.0 ** 30 if o[r] % 2 == 0 else 2.0 ** -30
    x = x[:, :, None, :, None] * np.ones((1, 1, 16, 1, 4))
    w = rng.choice([-1.0, 1.0], (N, 8, 16, 1, 8, 2, 1, 4)) * np.full((1, 1, 1, 4, 1, 1, 8, 1), least)
    return {"x": x.astype(np.float32).reshape(N, 128, 4 * C).astype(BF), "u": u.reshape(N, 128, 512), "v": v.astype(np.float32).astype(BF), **weights(rng, w.astype(np.float32).astype(BF))}
def setup_inputs_spread(rng):
    d = setup_inputs(rng)
    d["x"] = wide(rng, N, 128, 4 * C, cols=2)
    return d
def check_inputs(d):
    b = []
    for k in ("x", "u", "v"):
        a = np.abs(d[k].astype(np.float32))
        if not (np.isfinite(a).all() and ((a == 0) | (a >= 2.0 ** -30) & (a <= 2.0 ** 30)).all()): b.append("a value of " + k)
    none, least, most = [emit(mx_ref.quantize(np.full((128, 16), k, np.float32).astype(BF)))[1][0, 0] for k in (0.0, 2.0 ** -30, 2.0 ** 30)]
    top = 0.0
    for r in range(N):
        if ((d["wc"][r] == 0x7F) | (d["wc"][r] == 0xFF)).any(): b.append("wc: a code that is no number")
        s = mx_ref.live(d["ws"][r])
        if ((s != none) & ((s < least) | (s > most))).any(): b.append("ws: a scale out of range")
        top = max(top, float(np.abs(decode(pk(d["wc"][r], d["ws"][r]))).max()))
    if not float(np.abs(d["x"].astype(np.float32)).max()) * (1.0 + 32.0 * top) * (1.0 + 32.0 * top) * (1.0 + 32.0 * top) <= 2.0 ** 30: b.append("x and W: too large together")
    return b
def reference(x, u, v, wc, ws):
    qu = [mx_ref.quantize(u[r]) for r in range(N)]
    lay = [pk(wc[r], ws[r]) for r in range(N)]
    now = [x[r] for r in range(N)]
    place = np.zeros((N, 8 * C), np.int64)
    for m in MASK:
        seats, made = [], []
        for r in range(N):
            q = mx_ref.quantize(now[r])
            own = decode(q).astype(BF).reshape(8, 16, C, 4)
            s = mx_ref.matmul(qu[r], q)[::16] + np.float32(0.0)
            o = np.argsort(-s.reshape(-1), kind="stable")
            place[r, o] = np.arange(8 * C)
            t = own[o // C, :, o % C].reshape(C, 8, 16, 4).transpose(1, 2, 0, 3)
            seats.append(mx_ref.quantize(np.ascontiguousarray(t).reshape(128, 4 * C)))
        for r in range(N):
            q = join(pick(seats[r ^ m], np.arange(H)), pick(seats[r], np.arange(H, C)))
            a = decode(q)
            t = tile([np.maximum(mx_ref.matmul(pick(lay[r], np.arange(128 * b, 128 * b + 128)), q), np.float32(0.0)) * np.float32(0.03125) + a[:, b::4] for b in range(4)])
            n = place[r].reshape(8, C)
            home = t.reshape(8, 16, C, 4)[n % 8, :, n // 8]
            made.append(np.ascontiguousarray(home.transpose(0, 2, 1, 3)).reshape(128, 4 * C))
        now = made
    y, pl = np.zeros((N, 128, C), np.float32), np.zeros((N, 8, C), np.float32)
    oc, osc = np.zeros((N, 128, 4 * C), np.uint8), np.zeros((N, 16, C), np.uint8)
    for r in range(N):
        q = mx_ref.quantize(now[r])
        y[r] = mx_ref.matmul(mx_ref.quantize(v[r]), q)
        pl[r] = place[r].reshape(8, C)
        oc[r], osc[r] = emit(q)
    return {"y": y, "pl": pl, "oc": oc, "osc": osc}

import numpy as np
from concourse.bass import DstId, RemoteDMATransfer
from concourse.mybir import dt, AluOpType, AxisListType, ActivationFunctionType

A = AluOpType
F = ActivationFunctionType
MASKS = [1, 2, 4]
SCRATCH = {"ps": ("psum", [128, 4096], "float32")}


def declare(dtype, text):
    for word in text.split():
        name, n = word.split(":")
        SCRATCH[name] = ("sbuf", [128, int(n)], dtype)


def declare_mx(text):
    for word in text.split():
        name, n = word.split(":")
        SCRATCH[name + "q"] = ("sbuf", [128, int(n)], "float8_e4m3fn_x4")
        SCRATCH[name + "s"] = ("sbuf", [128, int(n)], "uint8")


declare("float32", "iJ:256 pf:2 gf:2 gcol:2 hadd:2 rm:2 qm:8 numb:16 Vv:256 sc:16 nsc:16 sb:2048 rr:16 junk:128 rn:16"
        " scw:2048 lraw:128 a64:64 a32:32 rel:512 ysb:256 plsb:128")
declare("int32", "pI:2 gI:2 rI:2 lu32:64 pi:16 dg:64 h1:16 h2:16 h3:16 h4:16 h5:16 i1:16 i2:16")
declare("uint16", "lu:64 offp:16 offh:16 offt:16")
declare("bfloat16", "eb:2048 e4:512 sel:560 wp:960 wh:960 pm:512 ut:512 vt:512 xt:1024 dgb:64 rt:568 du:512 fw:8192 tw:8192 tt:1024"
        " md0:2048 md1:2048 md2:2048 md3:2048 ma0:2048 ma1:2048 ma2:2048 ma3:2048 tm0:2048 tm1:2048 tm2:2048 tm3:2048")
declare_mx("eb:512 e4:128 sel:140 wp:240 wh:240 pm:128 u:128 ub:1024 v:128 lw:1024 ew:1024 x:256 r:142 du:128"
           " m0:512 m1:512 m2:512 m3:512 ta:256 tb:256 tc:256 la0:128 la1:128 la2:128")
SEMAPHORES = ["cV", "cS", "cT", "cG", "lx", "lu", "lw", "le", "lv", "dF", "dT", "dL", "st", "sent", "arr0", "arr1", "arr2"]

OWN = 2
ROWS_S = [1, 3, 6, 9, 12, 14]


def rank_program(g, core, T, topo):
    rank = T.rank_of(core)
    if rank is None:
        return
    eng = {"V": g.vector, "S": g.scalar, "T": g.tensor, "G": g, "Y": g.sync}
    count = {s: 0 for s in SEMAPHORES}
    waited = {}
    hist = {}

    def v(name, lo=None, hi=None, step=1, p0=0, p1=128):
        if lo is None:
            lo, hi = 0, SCRATCH[name][1][1]
        ap = T[name][p0:p1, lo:hi:step] if step != 1 else T[name][p0:p1, lo:hi]
        return (ap, [(name, lo, hi, step, p0, p1)])

    def ind(win, off):
        return (win[0].indirect(off[0]), win[1] + off[1])

    def words(w):
        return (w[0].bitcast(dt.uint32), w[1])

    def octets(w):
        return (w[0].bitcast(dt.uint8), w[1])

    def ext(ap):
        return (ap, [])

    def meet(a, b):
        if a[0] == "ps":
            return a[1] // 512 <= (b[2] - 1) // 512 and b[1] // 512 <= (a[2] - 1) // 512
        if a[1] >= b[2] or b[1] >= a[2] or a[4] >= b[5] or b[4] >= a[5]:
            return False
        return not (a[3] == b[3] and a[3] > 1 and (a[1] - b[1]) % a[3])

    def need(q, tok):
        if waited.get((q, tok[0]), 0) < tok[1]:
            eng[q].wait_ge(T.sem[tok[0]], tok[1])
            waited[(q, tok[0])] = tok[1]

    def order(q, ins, outs, isdma):
        toks = {}
        for kind, views in (("r", ins), ("w", outs)):
            for w in views:
                for reg in w[1]:
                    for (r2, k2, q2, d2, tok) in hist.get(reg[0], []):
                        if not meet(reg, r2):
                            continue
                        if q2 == q and not isdma and not d2:
                            if kind == k2 == "r" or q == "T":
                                continue
                        elif kind == "r" and k2 == "r" and reg[0] != "ps":
                            continue
                        toks[tok[0]] = max(toks.get(tok[0], 0), tok[1])
        for s in toks:
            need(q, (s, toks[s]))

    def note(q, ins, outs, isdma, tok):
        for kind, views in (("r", ins), ("w", outs)):
            for w in views:
                for reg in w[1]:
                    h = hist.setdefault(reg[0], [])
                    h[:] = [e for e in h if not (e[0] == reg and e[1] == kind and e[2] == q and e[4][0] == tok[0])]
                    if kind == "w" and reg[0] != "ps":
                        h[:] = [e for e in h if not (reg[3] == 1 and e[0][1] >= reg[1] and e[0][2] <= reg[2] and e[0][4] >= reg[4] and e[0][5] <= reg[5])]
                    h.append((reg, kind, q, isdma, tok))

    def run(q, call, outs, ins):
        order(q, ins, outs, False)
        s = "c" + q
        count[s] += 1
        call(eng[q]).then_inc(T.sem[s], 1)
        note(q, ins, outs, False, (s, count[s]))

    def dmas(sem, moves):
        tok = (sem, count[sem] + 16 * len(moves))
        for q, o, i in moves:
            order(q, [i], [o], True)
        for q, o, i in moves:
            eng[q].dma_start(o[0], i[0]).then_inc(T.sem[sem], 16)
        count[sem] = tok[1]
        for q, o, i in moves:
            note(q, [i], [o], True, tok)

    def act(o, i, func, bias=None, scale=None, acc=None):
        kw, ins, outs = {}, [i], [o]
        for key, a in (("bias", bias), ("scale", scale)):
            if isinstance(a, tuple):
                ins = ins + [a]
                kw[key] = a[0]
            elif a is not None:
                kw[key] = a
        if acc is not None:
            kw["accum_out"] = acc[0]
            outs = outs + [acc]
        run("S", lambda e: e.activation(o[0], i[0], func, **kw), outs, ins)

    def copy(q, o, i):
        if q == "V":
            run(q, lambda e: e.tensor_copy(o[0], i[0]), [o], [i])
        else:
            act(o, i, F.Copy)

    def ts(o, i, s1, op, s2=None, op1=None):
        ins = [i] + [s for s in (s1, s2) if isinstance(s, tuple)]
        a1 = s1[0] if isinstance(s1, tuple) else s1
        a2 = s2[0] if isinstance(s2, tuple) else s2
        if op1 is None:
            run("V", lambda e: e.tensor_scalar(o[0], i[0], a1, None, op), [o], ins)
        else:
            run("V", lambda e: e.tensor_scalar(o[0], i[0], a1, a2, op, op1), [o], ins)

    def tt(o, a, b, op):
        run("V", lambda e: e.tensor_tensor(o[0], a[0], b[0], op), [o], [a, b])

    def fill(o, c):
        run("V", lambda e: e.memset(o[0], c), [o], [])

    def mx(name, lo=None, hi=None):
        return (v(name + "q", lo, hi), v(name + "s", lo, hi))

    def quant(o, i):
        run("V", lambda e: e.quantize_mx(o[0][0], o[1][0], i[0]), [o[0], o[1]], [i])

    def mm(o, a, b, start=True, stop=True):
        run("T", lambda e: e.matmul_mx(o[0], a[0][0], a[1][0], b[0][0], b[1][0], start, stop), [o], [a[0], a[1], b[0], b[1]])

    def iota(o, pattern, cm=0):
        if SCRATCH[o[1][0][0]][2] == "int32":
            run("G", lambda e: e.iota(o[0], pattern, 0, cm), [o], [])
        else:
            run("G", lambda e: e.iota(o[0], pattern, 0, cm, allow_small_or_imprecise_dtypes=True), [o], [])

    def later(o):
        run("G", lambda e: e.affine_select(o[0], o[0], [[1, 128]], A.is_gt, 0.0, 0, -1), [o], [o])

    def bank(b, lo, hi, step=1):
        return v("ps", 512 * b + lo, 512 * b + hi, step)

    def turn(sem, w, lo, hi, first=1):
        dmas(sem, [("Y", v(w, 1024 * k + lo, 1024 * k + hi, 1, d0, d1), v(w, lo, hi, 1, s0, s0 + d1 - d0))
                   for k in range(first, 8) for d0, d1, s0 in ((0, 128 - 16 * k, 16 * k), (128 - 16 * k, 128, 0))])

    pf, iJ = v("pf", 0, 1), v("iJ")
    dmas("lx", [("Y", v("xt"), ext(T.x[:]))])
    dmas("lu", [("S", v("ut"), ext(T.u[:]))])
    dmas("lv", [("Y", v("vt"), ext(T.v[:]))])
    dmas("lw", [("Y", octets(v("lwq", 128 * j, 128 * j + 128)), ext(T.wc[:, 512 * (j // 2):512 * (j // 2) + 512])) for j in range(8)]
         + [("Y", v("lws", 128 * j, 128 * j + 128), ext(T.ws[:, 128 * (j // 2):128 * (j // 2) + 128])) for j in range(8)])
    iota(v("pI", 0, 1), [[1, 1]], 1)
    iota(iJ, [[1, 256]])
    iota(v("lu32"), [[16, 8], [0, 8]])
    iota(v("numb"), [[128, 16]], 1)
    for t in range(1, 4):
        for name in ("md%d" % t, "tm%d" % t):
            iota(v(name, 0, 512), [[0, 512]])
    copy("V", pf, v("pI", 0, 1))
    ts(v("gI", 0, 1), v("pI", 0, 1), 4, A.arith_shift_right)
    ts(v("rI", 0, 1), v("pI", 0, 1), 15, A.bitwise_and)
    fill(v("eb"), 0.0)
    copy("V", v("lu"), v("lu32"))
    for b in range(4):
        ts(v("eb", 512 * b + b, 512 * b + 512, 4), v("iJ", 0, 128), pf, A.is_equal)
    quant(mx("eb"), v("eb"))
    for t in range(4):
        ts(v("e4", t, 512, 4), v("iJ", 0, 128), pf, A.is_equal)
        ts(v("sel", t, 560, 4), v("iJ", 0, 140), float(12 + t), A.is_equal)
    quant(mx("e4"), v("e4"))
    quant(mx("sel"), v("sel"))
    quant(mx("u"), v("ut"))
    for h in range(8):
        act(v("scw", 256 * h, 256 * h + 256), iJ, F.Identity, bias=1024.0 * h, scale=0.0)
    act(v("ubs"), ind(v("us"), v("lu")), F.Copy)
    copy("V", words(v("ubq")), ind(words(v("uq")), v("lu")))
    quant(mx("x"), v("xt"))

    def spread_of(name, w):
        for t in range(4):
            ts(v(name, t, 960, 4), v("iJ", 0, 240), v("rm", 0, 1), A.is_equal, w[t], A.mult)
        quant(mx(name), v(name))

    def constants1():
        copy("V", v("gf", 0, 1), v("gI", 0, 1))
        ts(v("gcol", 0, 1), v("gI", 0, 1), 1024.0, A.mult)
        ts(v("rm", 0, 1), v("rI", 0, 1), 112.0, A.add)
        ts(v("qm"), v("iJ", 0, 8), v("gf", 0, 1), A.is_equal)
        ts(v("Vv"), iJ, v("gcol", 0, 1), A.add)
        spread_of("wp", (256.0, 16.0, 1.0, 8.0))
        fill(v("rt", 512, 568), 0.0)

    def constants2():
        ts(v("hadd", 0, 1), v("gI", 0, 1), -256.0, A.mult, 2048.0, A.add)
        spread_of("wh", (256.0, 1.0, 16.0, 128.0))
        for t, w in enumerate((1.0, 8.0, 128.0, 1024.0)):
            ts(v("pm", t, 512, 4), v("iJ", 0, 128), pf, A.is_equal, w, A.mult)
        quant(mx("pm"), v("pm"))
        fill(v("du"), 0.0)
        quant(mx("v"), v("vt"))

    CB, RB = 4, (5, 6, 7)

    def compare():
        state = {"V": 0.0, "S": 0.0, "mq": 0, "rb": 0, "c": 0}
        quanta, sums = [], []
        rows = {"V": [k for k in range(16) if k not in ROWS_S], "S": list(ROWS_S)}

        def us(n):
            return n * 0.00095 + 0.07

        def pieces(k):
            ch, t = k // 4, k % 4
            if t == 0:
                return [(0, 512 * (4 - ch), 1, 512 * ch)]
            a = [(x, 512, 4, 512 * ch + x) for x in range(t, 4)]
            return a + ([(512, 512 * (4 - ch), 1, 512 * (ch + 1))] if ch < 3 else [])

        def row(q, k):
            t, n = k % 4, 512 * (4 - k // 4)
            name = ("md%d" if q == "V" else "tm%d") % t
            for i, (lo, hi, step, src) in enumerate(pieces(k)):
                o, s = v(name, lo, hi, step), v("sb", src, src + hi - lo, step)
                if q == "V":
                    ts(o, s, v("sc", k, k + 1), A.is_gt)
                else:
                    act(o, s, F.Relu, bias=v("nsc", k, k + 1))
                state[q] += us((hi - lo) / step)
                if i == 0:
                    later(v(name, t, 512, 4))
            if q == "V":
                quanta.append((state["V"] + 0.6, k, name))
            else:
                act(v("ma%d" % t, 0, n), v(name, 0, n), F.Sign, acc=v("rr", k, k + 1))
                state["S"] += us(n)
                quanta.append((state["S"] + 0.2, k, "ma%d" % t))

        def pack(k, name):
            ch, m = k // 4, "m%d" % state["mq"]
            state["mq"] = (state["mq"] + 1) % 4
            n = 4 - ch
            quant(mx(m, 0, 128 * n), v(name, 0, 512 * n))
            state["V"] += 512 * n * 0.00023 + 0.06
            if name[:2] == "md":
                b = RB[state["rb"]]
                state["rb"] = (state["rb"] + 1) % 3
                for j in range(n):
                    mm(bank(b, 0, 128), mx("e4"), mx(m, 128 * j, 128 * j + 128), j == 0, j == n - 1)
                sums.append((state["V"] + 0.3 + 0.1 * n, k, b))
            for j in range(n):
                w = 12 - 4 * (ch + j)
                mm(bank(CB, 0, 128), mx(m, 128 * j, 128 * j + 128), mx("sel", w, w + 128), state["c"] == 0, state["c"] == 39)
                state["c"] += 1

        while rows["V"] or rows["S"] or quanta or sums:
            if (rows["V"] or quanta) and (not (rows["S"] or sums) or state["V"] <= state["S"]):
                ready = [e for e in quanta if e[0] <= state["V"]]
                if not ready and not rows["V"]:
                    ready = [min(quanta)]
                    state["V"] = max(state["V"], ready[0][0])
                if ready:
                    e = min(ready)
                    quanta.remove(e)
                    pack(e[1], e[2])
                else:
                    row("V", rows["V"].pop(0))
            else:
                ready = [e for e in sums if e[0] <= state["S"]]
                if not ready and not rows["S"]:
                    ready = [min(sums)]
                    state["S"] = max(state["S"], ready[0][0])
                if ready:
                    e = min(ready)
                    sums.remove(e)
                    act(v("junk"), bank(e[2], 0, 128), F.Copy, acc=v("rr", e[1], e[1] + 1))
                    state["S"] += us(128)
                else:
                    row("S", rows["S"].pop(0))

    for r, m in enumerate(MASKS):
        peer = T.cores[rank ^ m]
        rid, pid, _ = topo.addr(peer)
        engines = topo.mask(core, peer)
        neng = len(topo.engines(core, peer))
        for h in range(2):
            mm(bank(4 + h, 0, 128), mx("x", 128 * h, 128 * h + 128), mx("u"))
            copy("V", v("sc", h, 16, 2), bank(4 + h, 0, 128, 16))
        for k in range(8):
            mm(bank(k % 4, 0, 256), mx("ub", 128 * k, 128 * k + 128), mx("x"))
            for h in range(2):
                t = 2 * (k % 2) + h
                copy("VS"[k % 2], v("sb", 512 * (k // 2) + t, 512 * (k // 2) + 512, 4), bank(k % 4, 128 * h, 128 * h + 128))
        act(v("nsc"), v("sc"), F.Copy, scale=-1.0)
        for b in range(4):
            bk = (6, 7, 4, 5)[b]
            mm(bank(bk, 0, 256), mx("eb", 128 * b, 128 * b + 128), mx("x"))
            copy("VS"[b % 2], v("fw", 256 * b, 256 * b + 256), bank(bk, 0, 256))
        turn("dF", "fw", 0, 1024)
        if r == 0:
            dmas("le", [("Y", octets(v("ewq", 128 * j, 128 * j + 128)), octets(v("ebq", 128 * (j // 2), 128 * (j // 2) + 128))) for j in range(8)]
                 + [("Y", v("ews", 128 * j, 128 * j + 128), v("ebs", 128 * (j // 2), 128 * (j // 2) + 128)) for j in range(8)])
            constants1()
        compare()
        tt(v("rn"), v("numb"), v("rr"), A.add)
        tt(v("pi"), v("rn"), bank(CB, 0, 16), A.subtract)
        ts(v("dg", 0, 64, 4), v("pi"), 7, A.bitwise_and)
        ts(v("dg", 1, 64, 4), v("pi"), 3, A.arith_shift_right, 15, A.bitwise_and)
        ts(v("dg", 2, 64, 4), v("pi"), 7, A.arith_shift_right, 7, A.bitwise_and)
        ts(v("dg", 3, 64, 4), v("pi"), 10, A.arith_shift_right)
        copy("V", v("dgb"), v("dg"))
        for q in range(8):
            o, s = v("rt", 64 * q, 64 * q + 64), v("qm", q, q + 1)
            if q % 2:
                act(o, v("dgb"), F.Copy, scale=s)
            else:
                ts(o, v("dgb"), s, A.mult)
        quant(mx("r"), v("rt"))
        for k in range(8):
            mm(bank(0, 0, 128), mx("wp", 112 - 16 * k, 240 - 16 * k), mx("r", 2 * k, 2 * k + 128), k == 0, k == 7)
        for h in range(2):
            copy("V", v("offp", 8 * h, 8 * h + 8), bank(0, h, 128, 16))
        copy("V", ind(v("scw"), v("offp")), v("Vv"))
        dmas("dL", [("YS"[k % 2], v("lraw", 16 * k, 16 * k + 16), v("scw", 0, 2048, 1, 16 * k, 16 * k + 1)) for k in range(8)])
        if r == 0:
            constants2()
        for k in range(8):
            mm(bank(1, 0, 128), mx("wh", 112 - 16 * k, 240 - 16 * k), mx("r", 2 * k, 2 * k + 128), k == 0, k == 7)
        for h in range(2):
            ts(v("h1", 8 * h, 8 * h + 8), bank(1, h, 128, 16), v("hadd", 0, 1), A.add)
        ts(v("h2"), v("h1"), 127, A.bitwise_and)
        ts(v("h3"), v("h1"), 7, A.arith_shift_right, 15, A.bitwise_and)
        ts(v("h4"), v("h3"), 512.0, A.mult)
        tt(v("h5"), v("h4"), v("h2"), A.add)
        copy("V", v("offh"), v("h5"))
        if r == 2:
            copy("S", v("du", 0, 64), v("dgb"))
            quant(mx("du"), v("du"))
            mm(bank(2, 0, 128), mx("du"), mx("pm"))
            copy("S", v("plsb"), bank(2, 0, 128))
            dmas("st", [("Y", ext(T.pl[:]), v("plsb", 0, 128, 1, 0, 16))])
        tt(v("a64"), v("lraw", 0, 64), v("lraw", 64, 128), A.add)
        tt(v("a32"), v("a64", 0, 32), v("a64", 32, 64), A.add)
        tt(v("i1"), v("a32", 0, 16), v("a32", 16, 32), A.add)
        ts(v("i2"), v("i1"), 8191, A.bitwise_and)
        copy("V", v("offt"), v("i2"))
        for b in range(4):
            copy("VS"[b % 2], v("tt", b, 1024, 4), ind(v("fw", 256 * b, 256 * b + 7424), v("offt")))
        tn, la, arr = "t" + "abc"[r], "la%d" % r, "arr%d" % r
        for h in range(2):
            quant(mx(tn, 128 * h, 128 * h + 128), v("tt", 512 * h, 512 * h + 512))
            if h == 0:
                q, s = mx(tn, 0, 128)
                order("G", [q, s], [], True)
                g.remote_dma(octets(v(la + "q"))[0], octets(q)[0], T.sem[arr], T.sem.sent, pid, rid, engines)
                g.remote_dma(v(la + "s")[0], s[0], T.sem[arr], T.sem.sent, pid, rid, engines)
                count["sent"] += 2 * neng
                count[arr] += 2 * neng
                note("G", [], [v(la + "q"), v(la + "s")], True, (arr, count[arr]))
                if r < 2:
                    iota(v("scw"), [[1024, 8], [0, 256]])
        for h in (1, 0):
            side = mx(tn, 128, 256) if h else mx(la)
            for k in range(8 if h == 0 else 1 + OWN):
                for b in range(4):
                    w, o = 256 * b + 16 * k, 1024 * k + 512 * h + 128 * b
                    x = v("rel", 128 * b, 128 * b + 128)
                    mm(bank(b, 0, 128), mx("lw", w, w + 128), side)
                    mm(bank(4 + b, 0, 128), mx("ew", w, w + 128), side)
                    act(x, bank(b, 0, 128), F.Relu, scale=0.03125)
                    tt(v("tw", o, o + 128), x, bank(4 + b, 0, 128), A.add)
                if h and k == 0:
                    turn("dT", "tw", 512, 1024, 1 + OWN)
        for b in range(4):
            copy("VS"[b % 2], v("xt", b, 1024, 4), ind(v("tw", 128 * b, 128 * b + 7808), v("offh")))
        quant(mx("x"), v("xt"))
    mm(bank(0, 0, 256), mx("v"), mx("x"))
    copy("S", v("ysb"), bank(0, 0, 256))
    dmas("st", [("Y", ext(T.oc[:]), octets(v("xq"))), ("S", ext(T.y[:]), v("ysb"))]
         + [("YS"[k % 2], ext(T.osc[4 * k:4 * k + 4, 0:256]), v("xs", 0, 256, 1, 32 * k, 32 * k + 4)) for k in range(4)])
    for s in SEMAPHORES:
        need("G", (s, count[s]))
